import numpy as np
import ml_dtypes


def mxq(x, axis, fmt="e4m3"):
    dtype, down = {"e4m3": (ml_dtypes.float8_e4m3fn, 7), "e5m2": (ml_dtypes.float8_e5m2, 14)}[fmt]
    v = np.moveaxis(np.asarray(x, np.float32).astype(ml_dtypes.bfloat16).astype(np.float64), axis, -1)
    blocks = v.reshape(v.shape[:-1] + (-1, 32))
    amax = np.abs(blocks).max(-1, keepdims=True)
    byte = np.maximum(np.where(amax > 0, np.frexp(amax)[1] - 1 + 127, 0) - down, 1)
    scale = np.exp2(byte - 127.0)
    codes = (blocks / scale).astype(np.float32).astype(dtype).astype(np.float64)
    return np.moveaxis((codes * scale).reshape(v.shape), -1, axis)


WIDE = False


def mx_kscale(k):
    if not WIDE:
        return np.ones(k)
    levels = np.array([10, -10, 5, -5, 0])
    if k % 512:
        return np.exp2(np.random.permutation(np.resize(levels, k // 32))).repeat(32)
    a = np.empty((k // 512, 16))
    for p in range(k // 512):
        a[p, :8] = np.random.permutation(np.resize(levels, 8))
        for g in range(8):
            far = levels[np.abs(levels - a[p, g]) >= 10]
            a[p, g + 8] = far[np.random.randint(len(far))]
    return np.exp2(a.ravel()).repeat(32)


def f64(x):
    return np.asarray(x).astype(np.float64)


def striped(idx):
    return np.tile(idx.reshape(-1, 16).T, (8, 1)).astype(np.uint16)


def unstriped(offs):
    return offs[:16].T.reshape(-1).astype(np.int64)


def silu(v):
    return v / (1.0 + np.exp(-np.maximum(v, -700.0)))


K, T, E, C, H, N = 512, 1024, 16, 128, 512, 128


def by_expert(wq, xq):
    return np.concatenate([wq[e].T @ xq[:, e * C:(e + 1) * C] for e in range(E)], axis=1)


def setup_inputs():
    n = np.random.standard_normal
    s = mx_kscale(K)[:, None]
    u = mx_kscale(H)
    first = np.random.permutation(np.repeat(np.arange(E), T // E))
    second = (first + 1 + np.random.permutation(np.repeat(np.arange(E - 1), -(-T // (E - 1)))[:T])) % E
    while np.bincount(second, minlength=E).max() != T // E:
        load = np.bincount(second, minlength=E); hi, lo = int(load.argmax()), int(load.argmin())
        t = np.flatnonzero((second == hi) & (first != lo))[0]; second[t] = lo
    slot_token = np.empty(E * C, np.int64); pos = np.empty((2, T), np.int64); fill = np.zeros(E, np.int64)
    place = np.stack([np.random.permutation(C) for _ in range(E)])
    for r, deal in enumerate((first, second)):
        for t in np.random.permutation(T):
            e = deal[t]; j = e * C + place[e, fill[e]]; fill[e] += 1; slot_token[j] = t; pos[r, t] = j
    g = np.random.uniform(0.2, 0.8, T)
    return {
        "xT": (n((K, T)) * s).astype(np.float32),
        "w1": (n((E, K, H)) / np.sqrt(K) / s[None]).astype(np.float32),
        "w3": (n((E, K, H)) / np.sqrt(K) / s[None] * u[None, None, :]).astype(np.float32),
        "w2": (n((E, H, N)) / np.sqrt(H) / u[None, :, None]).astype(np.float32),
        "gate": np.stack([np.tile(g, (N, 1)), np.tile(1.0 - g, (N, 1))]).astype(np.float32),
        "offs": striped(slot_token),
        "pos1": striped(pos[0]),
        "pos2": striped(pos[1]),
    }


def reference(xT, w1, w3, w2, gate, offs, pos1, pos2):
    idx = unstriped(offs)
    xq = mxq(f64(xT)[:, idx], 0, "e4m3")
    h = silu(by_expert(mxq(f64(w1), 1, "e4m3"), xq))
    h = h * by_expert(mxq(f64(w3), 1, "e4m3"), xq)
    y = by_expert(mxq(f64(w2), 1, "e4m3"), mxq(h, 0, "e4m3"))
    return f64(gate[0]) * y[:, unstriped(pos1)] + f64(gate[1]) * y[:, unstriped(pos2)]

@@ -1,0 +1,278 @@
+from contextlib import ExitStack
+
+import concourse.mybir as mybir
+
+K, T, E, C, H, N = 512, 1024, 16, 128, 512, 128
+FLOPS = 2 * E * C * (2 * K * H + H * N)
+
+F32 = mybir.dt.float32
+BF16 = mybir.dt.bfloat16
+U32 = mybir.dt.uint32
+U16 = mybir.dt.uint16
+U8 = mybir.dt.uint8
+FP8X4 = mybir.dt.float8_e4m3fn_x4
+SILU = mybir.ActivationFunctionType.Silu
+MULT = mybir.AluOpType.mult
+ADD = mybir.AluOpType.add
+
+P = 128
+RAW_BUFS = 7
+W2_EARLY = 1
+W2_PIECES = ((0, 4), (4, 4), (8, 4), (12, 2), (14, 1), (15, 1))
+X_C_ON_VECTOR = 160
+W1_EXPERTS_ON_SCALAR = 2
+GATHER_SLOTS = 512
+OUT_CHUNK = 512
+
+
+def tile_routed_moe_kernel(tc, xT, w1, w3, w2, gate, offs, pos1, pos2, out):
+    nc = tc.nc
+    with ExitStack() as ctx:
+        lists = ctx.enter_context(tc.tile_pool(name="lists", bufs=1))
+        keep = ctx.enter_context(tc.tile_pool(name="keep", bufs=1))
+        raw = ctx.enter_context(tc.tile_pool(name="raw", bufs=RAW_BUFS))
+        stage = ctx.enter_context(tc.tile_pool(name="stage", bufs=3))
+        grouped = ctx.enter_context(tc.tile_pool(name="grouped", bufs=4))
+        fin = ctx.enter_context(tc.tile_pool(name="fin", bufs=1))
+        psum_a = ctx.enter_context(tc.psum_pool(name="psum_a", bufs=2))
+        psum_b = ctx.enter_context(tc.psum_pool(name="psum_b", bufs=4))
+        psum_y = ctx.enter_context(tc.psum_pool(name="psum_y", bufs=2))
+
+        offs_t = lists.tile([P, E * C // 16], U16, name="offs_t")
+        pos1_t = lists.tile([P, T // 16], U16, name="pos1_t")
+        pos2_t = lists.tile([P, T // 16], U16, name="pos2_t")
+
+        x_words = keep.tile([P, T], U32, name="x_words", align_bytes=64)
+        x_bytes = keep.tile([P, T], U8, name="x_bytes", align_bytes=64)
+        xg_words = keep.tile([P, E * C], U32, name="xg_words", align_bytes=64)
+        xg_bytes = keep.tile([P, E * C], U8, name="xg_bytes", align_bytes=64)
+        h_words = keep.tile([P, E * C], U32, name="h_words", align_bytes=64)
+        h_bytes = keep.tile([P, E * C], U8, name="h_bytes", align_bytes=64)
+        w2_words = keep.tile([P, E * N], U32, name="w2_words", align_bytes=64)
+        w2_bytes = keep.tile([P, E * N], U8, name="w2_bytes", align_bytes=64)
+        y_all = keep.tile([P, E * C], F32, name="y_all")
+        zero_col = keep.tile([P, 1], F32, name="zero_col")
+        silu_col = keep.tile([P, 1], F32, name="silu_col")
+
+        nc.vector.memset(zero_col[:], 0.0)
+        nc.scalar.activation(out=silu_col[:], in_=zero_col[:], func=SILU)
+        nc.gpsimd.memset(x_bytes[:], 0)
+
+        raw_tiles = {}
+
+        def load_x(i):
+            t = raw.tile([P, 4, T], F32, name="raw_x", tag="raw")
+            nc.sync.dma_start(out=t[:], in_=xT.rearrange("(p j) n -> p j n", j=4))
+            raw_tiles[("x", i)] = t
+
+        def load_pair(which, src, i):
+            t = raw.tile([P, 2, 4 * H], F32, name="raw_w", tag="raw")
+            nc.sync.dma_start(out=t[:], in_=src[2 * i : 2 * i + 2].rearrange("e (p j) c -> p e (j c)", j=4))
+            raw_tiles[(which, 2 * i)] = t[:, 0, :]
+            raw_tiles[(which, 2 * i + 1)] = t[:, 1, :]
+
+        def load_one(which, src, e):
+            t = raw.tile([P, 4 * H], F32, name="raw_w_one", tag="raw")
+            nc.sync.dma_start(out=t[:], in_=src[e].rearrange("(p j) c -> p (j c)", j=4))
+            raw_tiles[(which, e)] = t
+
+        def load_w2(i):
+            e0, n = W2_PIECES[i]
+            t = raw.tile([P, n, 4 * N], F32, name="raw_w2", tag="raw")
+            nc.sync.dma_start(out=t[:], in_=w2[e0 : e0 + n].rearrange("e (p j) n -> p e (j n)", j=4))
+            for k in range(n):
+                raw_tiles[("w2", e0 + k)] = (t, k)
+
+        def load_gate(i):
+            t = raw.tile([P, 2, T], F32, name="raw_gate", tag="raw")
+            nc.sync.dma_start(out=t[:], in_=gate.rearrange("g n t -> n g t"))
+            raw_tiles[("gate", i)] = t
+
+        jobs = [("x", 0)]
+        for i in range(E // 2 - 1):
+            jobs.append(("w1", i))
+            jobs.append(("w3", i))
+        for i in range(W2_EARLY):
+            jobs.append(("w2", i))
+        for e in (E - 2, E - 1):
+            jobs.append(("w1_one", e))
+            jobs.append(("w3_one", e))
+        for i in range(W2_EARLY, len(W2_PIECES)):
+            jobs.append(("w2", i))
+        jobs.append(("gate", 0))
+        issued = [0]
+
+        def issue_loads(upto):
+            while issued[0] < min(upto, len(jobs)):
+                kind, i = jobs[issued[0]]
+                if kind == "x":
+                    load_x(i)
+                elif kind == "w1":
+                    load_pair("w1", w1, i)
+                elif kind == "w3":
+                    load_pair("w3", w3, i)
+                elif kind == "w1_one":
+                    load_one("w1", w1, i)
+                elif kind == "w3_one":
+                    load_one("w3", w3, i)
+                elif kind == "w2":
+                    load_w2(i)
+                else:
+                    load_gate(i)
+                issued[0] += 1
+
+        nc.sync.dma_start(out=offs_t[:], in_=offs)
+        issue_loads(1)
+        nc.sync.dma_start(out=pos1_t[:], in_=pos1)
+        nc.sync.dma_start(out=pos2_t[:], in_=pos2)
+        issue_loads(RAW_BUFS)
+
+        x_grp = grouped.tile([P, T, 4], BF16, name="x_grp", tag="wg", align_bytes=64)
+        x_dst = x_grp.rearrange("p (c i) j -> p c j i", i=4)
+        x_src = raw_tiles[("x", 0)].rearrange("p j (c i) -> p c j i", i=4)
+        nc.vector.tensor_copy(out=x_dst[:, 0:128], in_=x_src[:, 0:128])
+        nc.vector.tensor_copy(out=x_dst[:, 128:X_C_ON_VECTOR], in_=x_src[:, 128:X_C_ON_VECTOR])
+        nc.scalar.copy(out=x_dst[:, X_C_ON_VECTOR:256], in_=x_src[:, X_C_ON_VECTOR:256])
+        for c in range(2):
+            nc.vector.quantize_mx(
+                out=x_words[:, 512 * c : 512 * (c + 1)].bitcast(FP8X4),
+                scales=x_bytes[:, 512 * c : 512 * (c + 1)],
+                in_=x_grp[:, 512 * c : 512 * (c + 1), :].rearrange("p n j -> p (n j)"),
+            )
+
+        def gather(q):
+            cols = slice(q * GATHER_SLOTS // 16, (q + 1) * GATHER_SLOTS // 16)
+            slots = slice(q * GATHER_SLOTS, (q + 1) * GATHER_SLOTS)
+            nc.vector.tensor_copy(out=xg_words[:, slots], in_=x_words[:].indirect(offs_t[:, cols]))
+            nc.vector.tensor_copy(out=xg_bytes[:, slots], in_=x_bytes[:].indirect(offs_t[:, cols]))
+
+        wg, wc, ws, a_ps, b_ps, sa, hb = {}, {}, {}, {}, {}, {}, {}
+
+        def interleave_w(e):
+            wg[e] = grouped.tile([P, 2, 4 * H], BF16, name="wg", tag="wg", align_bytes=64)
+            d1 = wg[e][:, 0, :].rearrange("p (t m j) -> p m j t", t=4, j=4)
+            s1 = raw_tiles[("w1", e)].rearrange("p (j m t) -> p m j t", j=4, t=4)
+            d3 = wg[e][:, 1, :].rearrange("p (t m j) -> p m j t", t=4, j=4)
+            s3 = raw_tiles[("w3", e)].rearrange("p (j m t) -> p m j t", j=4, t=4)
+            if e < W1_EXPERTS_ON_SCALAR:
+                nc.scalar.copy(out=d1, in_=s1)
+            else:
+                nc.vector.tensor_copy(out=d1, in_=s1)
+            nc.scalar.copy(out=d3, in_=s3)
+
+        def quant_w(e):
+            wc[e] = stage.tile([P, 2 * H], U32, name="wc", tag="wc", align_bytes=64)
+            ws[e] = stage.tile([P, 2 * H], U8, name="ws", tag="ws", align_bytes=64)
+            nc.vector.quantize_mx(out=wc[e][:].bitcast(FP8X4), scales=ws[e][:], in_=wg[e].rearrange("p a c -> p (a c)"))
+
+        def layer1(e):
+            slots = slice(e * C, (e + 1) * C)
+            a_ps[e] = psum_a.tile([P, 4, C], F32, name="a_ps", tag="a_ps")
+            b_ps[e] = psum_b.tile([P, 4, C], F32, name="b_ps", tag="b_ps")
+            for half, acc in ((0, a_ps[e]), (1, b_ps[e])):
+                for t in range(4):
+                    cols = slice(half * H + t * P, half * H + (t + 1) * P)
+                    nc.tensor.matmul_mx(
+                        out=acc[:, t, :],
+                        lhsT=wc[e][:, cols].bitcast(FP8X4),
+                        lhsT_scale=ws[e][:, cols],
+                        rhs=xg_words[:, slots].bitcast(FP8X4),
+                        rhs_scale=xg_bytes[:, slots],
+                        start=True,
+                        stop=True,
+                    )
+
+        def silu(e):
+            spent = raw_tiles[("w3", e + 1)][:, 0 : 4 * C] if e + 1 < E else raw_tiles[("w3", e)][:, 4 * C : 8 * C]
+            sa[e] = spent.rearrange("p (s t) -> p s t", t=4)
+            nc.scalar.activation(out=sa[e], in_=a_ps[e].rearrange("p t s -> p s t"), func=SILU)
+
+        def hidden_pair(i):
+            over = wg[2 * i + 2][:, 0, :] if 2 * i + 2 < E else wg[2 * i + 1][:, 1, :]
+            hb[i] = over[:, 0 : 8 * C]
+            for k in range(2):
+                e = 2 * i + k
+                nc.vector.tensor_tensor(
+                    out=hb[i][:, 4 * C * k : 4 * C * (k + 1)].rearrange("p (s t) -> p s t", t=4),
+                    in0=sa[e],
+                    in1=b_ps[e].rearrange("p t s -> p s t"),
+                    op=MULT,
+                )
+
+        def quant_h(i):
+            slots = slice(2 * i * C, (2 * i + 2) * C)
+            nc.vector.quantize_mx(out=h_words[:, slots].bitcast(FP8X4), scales=h_bytes[:, slots], in_=hb[i])
+
+        w2g = {}
+
+        def interleave_w2(i):
+            e0, n = W2_PIECES[i]
+            w2g[i] = stage.tile([P, n, 4 * N], BF16, name="w2g", tag="w2g", align_bytes=64)
+            t, k0 = raw_tiles[("w2", e0)]
+            nv = (n + 1) // 2
+            d = w2g[i].rearrange("p e (c i j) -> p e c j i", i=4, j=4)
+            s = t[:, k0 : k0 + n, :].rearrange("p e (j c i) -> p e c j i", j=4, i=4)
+            nc.vector.tensor_copy(out=d[:, 0:nv], in_=s[:, 0:nv])
+            if nv < n:
+                nc.scalar.copy(out=d[:, nv:n], in_=s[:, nv:n])
+
+        def layer2(i):
+            e0, n = W2_PIECES[i]
+            cols = slice(e0 * N, (e0 + n) * N)
+            nc.vector.quantize_mx(
+                out=w2_words[:, cols].bitcast(FP8X4), scales=w2_bytes[:, cols], in_=w2g[i].rearrange("p e c -> p (e c)")
+            )
+            y_ps = psum_y.tile([P, n * C], F32, name="y_ps", tag="y_ps")
+            for k in range(n):
+                e = e0 + k
+                sl = slice(e * C, (e + 1) * C)
+                nc.tensor.matmul_mx(
+                    out=y_ps[:, k * C : (k + 1) * C],
+                    lhsT=w2_words[:, sl].bitcast(FP8X4),
+                    lhsT_scale=w2_bytes[:, sl],
+                    rhs=h_words[:, sl].bitcast(FP8X4),
+                    rhs_scale=h_bytes[:, sl],
+                    start=True,
+                    stop=True,
+                )
+            nc.scalar.copy(out=y_all[:, e0 * C : (e0 + n) * C], in_=y_ps[:])
+
+        gather(0)
+        for step in range(E + 5):
+            issue_loads(step + RAW_BUFS - 1)
+            if step == E - 2:
+                for i in range(W2_EARLY):
+                    interleave_w2(i)
+            if step == E - 1:
+                for i in range(W2_EARLY):
+                    layer2(i)
+            if step < E:
+                interleave_w(step)
+            if step % 4 == 1 and step // 4 + 1 < 4:
+                gather(step // 4 + 1)
+            if 0 <= step - 1 < E:
+                quant_w(step - 1)
+                layer1(step - 1)
+            if 0 <= step - 2 < E:
+                silu(step - 2)
+            if step % 2 == 1 and 0 <= step - 3 < E:
+                hidden_pair((step - 3) // 2)
+            if step % 2 == 0 and 0 <= step - 4 < E:
+                quant_h((step - 4) // 2)
+
+        for i in range(W2_EARLY, len(W2_PIECES) + 1):
+            if i < len(W2_PIECES):
+                interleave_w2(i)
+            if i > W2_EARLY:
+                layer2(i - 1)
+
+        gate_t = raw_tiles[("gate", 0)]
+        g1 = fin.tile([P, T], F32, name="g1", tag="g1")
+        g2 = fin.tile([P, T], F32, name="g2", tag="g2")
+        res = fin.tile([P, T], F32, name="res", tag="res")
+        nc.vector.tensor_tensor(out=g1[:], in0=y_all[:].indirect(pos1_t[:]), in1=gate_t[:, 0, :], op=MULT)
+        nc.vector.tensor_tensor(out=g2[:], in0=y_all[:].indirect(pos2_t[:]), in1=gate_t[:, 1, :], op=MULT)
+        for c in range(T // OUT_CHUNK):
+            tok = slice(c * OUT_CHUNK, (c + 1) * OUT_CHUNK)
+            nc.vector.tensor_tensor(out=res[:, tok], in0=g1[:, tok], in1=g2[:, tok], op=ADD)
+            nc.sync.dma_start(out=out[:, tok], in_=res[:, tok])

@@ -17,8 +17,9 @@ ADD = mybir.AluOpType.add
 
 P = 128
 RAW_BUFS = 7
-W2_EARLY = 1
+PAIRED = 12
 W2_PIECES = ((0, 4), (4, 4), (8, 4), (12, 2), (14, 1), (15, 1))
+Y_WOVEN = 12
 X_C_ON_VECTOR = 160
 W1_EXPERTS_ON_SCALAR = 2
 GATHER_SLOTS = 512
@@ -33,10 +34,11 @@ def tile_routed_moe_kernel(tc, xT, w1, w3, w2, gate, offs, pos1, pos2, out):
         raw = ctx.enter_context(tc.tile_pool(name="raw", bufs=RAW_BUFS))
         stage = ctx.enter_context(tc.tile_pool(name="stage", bufs=3))
         grouped = ctx.enter_context(tc.tile_pool(name="grouped", bufs=4))
+        hidden = ctx.enter_context(tc.tile_pool(name="hidden", bufs=2))
         fin = ctx.enter_context(tc.tile_pool(name="fin", bufs=1))
         psum_a = ctx.enter_context(tc.psum_pool(name="psum_a", bufs=2))
-        psum_b = ctx.enter_context(tc.psum_pool(name="psum_b", bufs=4))
-        psum_y = ctx.enter_context(tc.psum_pool(name="psum_y", bufs=2))
+        psum_b = ctx.enter_context(tc.psum_pool(name="psum_b", bufs=2))
+        psum_y = ctx.enter_context(tc.psum_pool(name="psum_y", bufs=4))
 
         offs_t = lists.tile([P, E * C // 16], U16, name="offs_t")
         pos1_t = lists.tile([P, T // 16], U16, name="pos1_t")
@@ -59,73 +61,55 @@ def tile_routed_moe_kernel(tc, xT, w1, w3, w2, gate, offs, pos1, pos2, out):
         nc.gpsimd.memset(x_bytes[:], 0)
 
         raw_tiles = {}
-
-        def load_x(i):
-            t = raw.tile([P, 4, T], F32, name="raw_x", tag="raw")
-            nc.sync.dma_start(out=t[:], in_=xT.rearrange("(p j) n -> p j n", j=4))
-            raw_tiles[("x", i)] = t
-
-        def load_pair(which, src, i):
-            t = raw.tile([P, 2, 4 * H], F32, name="raw_w", tag="raw")
-            nc.sync.dma_start(out=t[:], in_=src[2 * i : 2 * i + 2].rearrange("e (p j) c -> p e (j c)", j=4))
-            raw_tiles[(which, 2 * i)] = t[:, 0, :]
-            raw_tiles[(which, 2 * i + 1)] = t[:, 1, :]
-
-        def load_one(which, src, e):
-            t = raw.tile([P, 4 * H], F32, name="raw_w_one", tag="raw")
-            nc.sync.dma_start(out=t[:], in_=src[e].rearrange("(p j) c -> p (j c)", j=4))
-            raw_tiles[(which, e)] = t
-
-        def load_w2(i):
-            e0, n = W2_PIECES[i]
-            t = raw.tile([P, n, 4 * N], F32, name="raw_w2", tag="raw")
-            nc.sync.dma_start(out=t[:], in_=w2[e0 : e0 + n].rearrange("e (p j) n -> p e (j n)", j=4))
-            for k in range(n):
-                raw_tiles[("w2", e0 + k)] = (t, k)
-
-        def load_gate(i):
-            t = raw.tile([P, 2, T], F32, name="raw_gate", tag="raw")
-            nc.sync.dma_start(out=t[:], in_=gate.rearrange("g n t -> n g t"))
-            raw_tiles[("gate", i)] = t
-
-        jobs = [("x", 0)]
-        for i in range(E // 2 - 1):
-            jobs.append(("w1", i))
-            jobs.append(("w3", i))
-        for i in range(W2_EARLY):
-            jobs.append(("w2", i))
-        for e in (E - 2, E - 1):
-            jobs.append(("w1_one", e))
-            jobs.append(("w3_one", e))
-        for i in range(W2_EARLY, len(W2_PIECES)):
-            jobs.append(("w2", i))
-        jobs.append(("gate", 0))
+        jobs = [("x", 0, -1)]
+        for i in range(PAIRED // 2):
+            jobs.append(("w1_pair", i, 2 * i + 1))
+            jobs.append(("w3_pair", i, 2 * i + 3))
+        for e in range(PAIRED, E):
+            jobs.append(("w1", e, e))
+            jobs.append(("w3", e, e + 2))
+        for i in range(len(W2_PIECES)):
+            jobs.append(("w2", i, E + 2))
+        jobs.append(("gate", 0, E + 2))
         issued = [0]
 
-        def issue_loads(upto):
-            while issued[0] < min(upto, len(jobs)):
-                kind, i = jobs[issued[0]]
-                if kind == "x":
-                    load_x(i)
-                elif kind == "w1":
-                    load_pair("w1", w1, i)
-                elif kind == "w3":
-                    load_pair("w3", w3, i)
-                elif kind == "w1_one":
-                    load_one("w1", w1, i)
-                elif kind == "w3_one":
-                    load_one("w3", w3, i)
-                elif kind == "w2":
-                    load_w2(i)
-                else:
-                    load_gate(i)
+        def load(kind, i):
+            if kind == "x":
+                t = raw.tile([P, 4, T], F32, name="raw_x", tag="raw")
+                nc.sync.dma_start(out=t[:], in_=xT.rearrange("(p j) n -> p j n", j=4))
+                raw_tiles[("x", 0)] = t
+            elif kind in ("w1_pair", "w3_pair"):
+                t = raw.tile([P, 2, 4 * H], F32, name="raw_w", tag="raw")
+                src = w1 if kind == "w1_pair" else w3
+                nc.sync.dma_start(out=t[:], in_=src[2 * i : 2 * i + 2].rearrange("e (p j) c -> p e (j c)", j=4))
+                raw_tiles[(kind[0:2], 2 * i)] = t[:, 0, :]
+                raw_tiles[(kind[0:2], 2 * i + 1)] = t[:, 1, :]
+            elif kind in ("w1", "w3"):
+                t = raw.tile([P, 4 * H], F32, name="raw_w_one", tag="raw")
+                src = w1 if kind == "w1" else w3
+                nc.sync.dma_start(out=t[:], in_=src[i].rearrange("(p j) c -> p (j c)", j=4))
+                raw_tiles[(kind, i)] = t
+            elif kind == "w2":
+                e0, n = W2_PIECES[i]
+                t = raw.tile([P, n, 4 * N], F32, name="raw_w2", tag="raw")
+                nc.sync.dma_start(out=t[:], in_=w2[e0 : e0 + n].rearrange("e (p j) n -> p e (j n)", j=4))
+                raw_tiles[("w2", i)] = t
+            else:
+                t = raw.tile([P, 2, T], F32, name="raw_gate", tag="raw")
+                nc.sync.dma_start(out=t[:], in_=gate.rearrange("g n t -> n g t"))
+                raw_tiles[("gate", 0)] = t
+
+        def issue_loads(step):
+            while issued[0] < len(jobs) and (issued[0] < RAW_BUFS or jobs[issued[0] - RAW_BUFS][2] < step):
+                load(jobs[issued[0]][0], jobs[issued[0]][1])
                 issued[0] += 1
 
         nc.sync.dma_start(out=offs_t[:], in_=offs)
-        issue_loads(1)
+        load("x", 0)
+        issued[0] = 1
         nc.sync.dma_start(out=pos1_t[:], in_=pos1)
         nc.sync.dma_start(out=pos2_t[:], in_=pos2)
-        issue_loads(RAW_BUFS)
+        issue_loads(-1)
 
         x_grp = grouped.tile([P, T, 4], BF16, name="x_grp", tag="wg", align_bytes=64)
         x_dst = x_grp.rearrange("p (c i) j -> p c j i", i=4)
@@ -146,10 +130,12 @@ def tile_routed_moe_kernel(tc, xT, w1, w3, w2, gate, offs, pos1, pos2, out):
             nc.vector.tensor_copy(out=xg_words[:, slots], in_=x_words[:].indirect(offs_t[:, cols]))
             nc.vector.tensor_copy(out=xg_bytes[:, slots], in_=x_bytes[:].indirect(offs_t[:, cols]))
 
-        wg, wc, ws, a_ps, b_ps, sa, hb = {}, {}, {}, {}, {}, {}, {}
+        wg, wc, ws, acc, sa, hb = {}, {}, {}, {}, {}, {}
 
         def interleave_w(e):
             wg[e] = grouped.tile([P, 2, 4 * H], BF16, name="wg", tag="wg", align_bytes=64)
+            wc[e] = stage.tile([P, 2 * H], U32, name="wc", tag="wc", align_bytes=64)
+            ws[e] = stage.tile([P, 2 * H], U8, name="ws", tag="ws", align_bytes=64)
             d1 = wg[e][:, 0, :].rearrange("p (t m j) -> p m j t", t=4, j=4)
             s1 = raw_tiles[("w1", e)].rearrange("p (j m t) -> p m j t", j=4, t=4)
             d3 = wg[e][:, 1, :].rearrange("p (t m j) -> p m j t", t=4, j=4)
@@ -160,61 +146,72 @@ def tile_routed_moe_kernel(tc, xT, w1, w3, w2, gate, offs, pos1, pos2, out):
                 nc.vector.tensor_copy(out=d1, in_=s1)
             nc.scalar.copy(out=d3, in_=s3)
 
-        def quant_w(e):
-            wc[e] = stage.tile([P, 2 * H], U32, name="wc", tag="wc", align_bytes=64)
-            ws[e] = stage.tile([P, 2 * H], U8, name="ws", tag="ws", align_bytes=64)
-            nc.vector.quantize_mx(out=wc[e][:].bitcast(FP8X4), scales=ws[e][:], in_=wg[e].rearrange("p a c -> p (a c)"))
-
-        def layer1(e):
+        def layer1(e, half):
+            cols = slice(half * H, (half + 1) * H)
+            nc.vector.quantize_mx(out=wc[e][:, cols].bitcast(FP8X4), scales=ws[e][:, cols], in_=wg[e][:, half, :])
             slots = slice(e * C, (e + 1) * C)
-            a_ps[e] = psum_a.tile([P, 4, C], F32, name="a_ps", tag="a_ps")
-            b_ps[e] = psum_b.tile([P, 4, C], F32, name="b_ps", tag="b_ps")
-            for half, acc in ((0, a_ps[e]), (1, b_ps[e])):
-                for t in range(4):
-                    cols = slice(half * H + t * P, half * H + (t + 1) * P)
-                    nc.tensor.matmul_mx(
-                        out=acc[:, t, :],
-                        lhsT=wc[e][:, cols].bitcast(FP8X4),
-                        lhsT_scale=ws[e][:, cols],
-                        rhs=xg_words[:, slots].bitcast(FP8X4),
-                        rhs_scale=xg_bytes[:, slots],
-                        start=True,
-                        stop=True,
-                    )
+            if half == 0:
+                acc[(e, half)] = psum_a.tile([P, 4, C], F32, name="a_ps", tag="a_ps")
+            else:
+                acc[(e, half)] = psum_b.tile([P, 4, C], F32, name="b_ps", tag="b_ps")
+            for t in range(4):
+                cols = slice(half * H + t * P, half * H + (t + 1) * P)
+                nc.tensor.matmul_mx(
+                    out=acc[(e, half)][:, t, :],
+                    lhsT=wc[e][:, cols].bitcast(FP8X4),
+                    lhsT_scale=ws[e][:, cols],
+                    rhs=xg_words[:, slots].bitcast(FP8X4),
+                    rhs_scale=xg_bytes[:, slots],
+                    start=True,
+                    stop=True,
+                )
 
         def silu(e):
-            spent = raw_tiles[("w3", e + 1)][:, 0 : 4 * C] if e + 1 < E else raw_tiles[("w3", e)][:, 4 * C : 8 * C]
-            sa[e] = spent.rearrange("p (s t) -> p s t", t=4)
-            nc.scalar.activation(out=sa[e], in_=a_ps[e].rearrange("p t s -> p s t"), func=SILU)
+            sa[e] = raw_tiles[("w3", e)][:, 0 : 4 * C].rearrange("p (s t) -> p s t", t=4)
+            nc.scalar.activation(out=sa[e], in_=acc[(e, 0)].rearrange("p t s -> p s t"), func=SILU)
 
-        def hidden_pair(i):
-            over = wg[2 * i + 2][:, 0, :] if 2 * i + 2 < E else wg[2 * i + 1][:, 1, :]
-            hb[i] = over[:, 0 : 8 * C]
-            for k in range(2):
-                e = 2 * i + k
-                nc.vector.tensor_tensor(
-                    out=hb[i][:, 4 * C * k : 4 * C * (k + 1)].rearrange("p (s t) -> p s t", t=4),
-                    in0=sa[e],
-                    in1=b_ps[e].rearrange("p t s -> p s t"),
-                    op=MULT,
-                )
+        def product(e):
+            if e % 2 == 0:
+                hb[e // 2] = hidden.tile([P, 8 * C], BF16, name="hb", tag="hb", align_bytes=64)
+            k = e % 2
+            nc.vector.tensor_tensor(
+                out=hb[e // 2][:, 4 * C * k : 4 * C * (k + 1)].rearrange("p (s t) -> p s t", t=4),
+                in0=sa[e],
+                in1=acc[(e, 1)].rearrange("p t s -> p s t"),
+                op=MULT,
+            )
 
         def quant_h(i):
             slots = slice(2 * i * C, (2 * i + 2) * C)
-            nc.vector.quantize_mx(out=h_words[:, slots].bitcast(FP8X4), scales=h_bytes[:, slots], in_=hb[i])
+            nc.vector.quantize_mx(out=h_words[:, slots].bitcast(FP8X4), scales=h_bytes[:, slots], in_=hb[i][:])
 
         w2g = {}
 
         def interleave_w2(i):
             e0, n = W2_PIECES[i]
             w2g[i] = stage.tile([P, n, 4 * N], BF16, name="w2g", tag="w2g", align_bytes=64)
-            t, k0 = raw_tiles[("w2", e0)]
             nv = (n + 1) // 2
             d = w2g[i].rearrange("p e (c i j) -> p e c j i", i=4, j=4)
-            s = t[:, k0 : k0 + n, :].rearrange("p e (j c i) -> p e c j i", j=4, i=4)
+            s = raw_tiles[("w2", i)].rearrange("p e (j c i) -> p e c j i", j=4, i=4)
             nc.vector.tensor_copy(out=d[:, 0:nv], in_=s[:, 0:nv])
             if nv < n:
                 nc.scalar.copy(out=d[:, nv:n], in_=s[:, nv:n])
+
+        def y_matmul(e, where):
+            sl = slice(e * C, (e + 1) * C)
+            nc.tensor.matmul_mx(
+                out=where,
+                lhsT=w2_words[:, sl].bitcast(FP8X4),
+                lhsT_scale=w2_bytes[:, sl],
+                rhs=h_words[:, sl].bitcast(FP8X4),
+                rhs_scale=h_bytes[:, sl],
+                start=True,
+                stop=True,
+            )
+
+        woven = []
+        for b in range(3):
+            woven.append(psum_y.tile([P, 4, C], F32, name="y_woven", tag="y_ps"))
 
         def layer2(i):
             e0, n = W2_PIECES[i]
@@ -222,48 +219,42 @@ def tile_routed_moe_kernel(tc, xT, w1, w3, w2, gate, offs, pos1, pos2, out):
             nc.vector.quantize_mx(
                 out=w2_words[:, cols].bitcast(FP8X4), scales=w2_bytes[:, cols], in_=w2g[i].rearrange("p e c -> p (e c)")
             )
-            y_ps = psum_y.tile([P, n * C], F32, name="y_ps", tag="y_ps")
-            for k in range(n):
-                e = e0 + k
-                sl = slice(e * C, (e + 1) * C)
-                nc.tensor.matmul_mx(
-                    out=y_ps[:, k * C : (k + 1) * C],
-                    lhsT=w2_words[:, sl].bitcast(FP8X4),
-                    lhsT_scale=w2_bytes[:, sl],
-                    rhs=h_words[:, sl].bitcast(FP8X4),
-                    rhs_scale=h_bytes[:, sl],
-                    start=True,
-                    stop=True,
-                )
-            nc.scalar.copy(out=y_all[:, e0 * C : (e0 + n) * C], in_=y_ps[:])
+            if e0 < Y_WOVEN:
+                for e in range(e0, e0 + n):
+                    y_matmul(e, woven[e % 3][:, e // 3, :])
+                if e0 + n == Y_WOVEN:
+                    for b in range(3):
+                        dst = y_all[:, 0 : Y_WOVEN * C].rearrange("p (k b c) -> p b k c", b=3, c=C)[:, b]
+                        nc.scalar.copy(out=dst, in_=woven[b][:])
+            else:
+                pool, tag = ((psum_y, "y_ps"), (psum_a, "a_ps"), (psum_b, "b_ps"))[i - 3]
+                y_ps = pool.tile([P, n * C], F32, name="y_last", tag=tag)
+                for k in range(n):
+                    y_matmul(e0 + k, y_ps[:, k * C : (k + 1) * C])
+                nc.scalar.copy(out=y_all[:, e0 * C : (e0 + n) * C], in_=y_ps[:])
 
         gather(0)
-        for step in range(E + 5):
-            issue_loads(step + RAW_BUFS - 1)
-            if step == E - 2:
-                for i in range(W2_EARLY):
-                    interleave_w2(i)
-            if step == E - 1:
-                for i in range(W2_EARLY):
-                    layer2(i)
+        for step in range(E + 2):
+            issue_loads(step)
             if step < E:
                 interleave_w(step)
             if step % 4 == 1 and step // 4 + 1 < 4:
                 gather(step // 4 + 1)
+            if step < E:
+                layer1(step, 0)
             if 0 <= step - 1 < E:
-                quant_w(step - 1)
-                layer1(step - 1)
+                silu(step - 1)
+                layer1(step - 1, 1)
             if 0 <= step - 2 < E:
-                silu(step - 2)
-            if step % 2 == 1 and 0 <= step - 3 < E:
-                hidden_pair((step - 3) // 2)
-            if step % 2 == 0 and 0 <= step - 4 < E:
-                quant_h((step - 4) // 2)
+                product(step - 2)
+                if step % 2 == 1:
+                    quant_h((step - 2) // 2)
+        issue_loads(E + 3)
 
-        for i in range(W2_EARLY, len(W2_PIECES) + 1):
+        for i in range(len(W2_PIECES) + 1):
             if i < len(W2_PIECES):
                 interleave_w2(i)
-            if i > W2_EARLY:
+            if i > 0:
                 layer2(i - 1)
 
         gate_t = raw_tiles[("gate", 0)]

@@ -19,11 +19,12 @@ P = 128
 RAW_BUFS = 7
 PAIRED = 12
 W2_PIECES = ((0, 4), (4, 4), (8, 4), (12, 2), (14, 1), (15, 1))
+W2_EXPERTS_ON_VECTOR = (2, 2, 2, 0, 1, 1)
 Y_WOVEN = 12
 X_C_ON_VECTOR = 160
 W1_EXPERTS_ON_SCALAR = 2
 GATHER_SLOTS = 512
-OUT_CHUNK = 512
+OUT_CHUNK = 256
 
 
 def tile_routed_moe_kernel(tc, xT, w1, w3, w2, gate, offs, pos1, pos2, out):
@@ -190,10 +191,11 @@ def tile_routed_moe_kernel(tc, xT, w1, w3, w2, gate, offs, pos1, pos2, out):
         def interleave_w2(i):
             e0, n = W2_PIECES[i]
             w2g[i] = stage.tile([P, n, 4 * N], BF16, name="w2g", tag="w2g", align_bytes=64)
-            nv = (n + 1) // 2
+            nv = W2_EXPERTS_ON_VECTOR[i]
             d = w2g[i].rearrange("p e (c i j) -> p e c j i", i=4, j=4)
             s = raw_tiles[("w2", i)].rearrange("p e (j c i) -> p e c j i", j=4, i=4)
-            nc.vector.tensor_copy(out=d[:, 0:nv], in_=s[:, 0:nv])
+            if nv > 0:
+                nc.vector.tensor_copy(out=d[:, 0:nv], in_=s[:, 0:nv])
             if nv < n:
                 nc.scalar.copy(out=d[:, nv:n], in_=s[:, nv:n])
 
@@ -231,7 +233,10 @@ def tile_routed_moe_kernel(tc, xT, w1, w3, w2, gate, offs, pos1, pos2, out):
                 y_ps = pool.tile([P, n * C], F32, name="y_last", tag=tag)
                 for k in range(n):
                     y_matmul(e0 + k, y_ps[:, k * C : (k + 1) * C])
-                nc.scalar.copy(out=y_all[:, e0 * C : (e0 + n) * C], in_=y_ps[:])
+                if e0 + n == E:
+                    nc.vector.tensor_copy(out=y_all[:, e0 * C : (e0 + n) * C], in_=y_ps[:])
+                else:
+                    nc.scalar.copy(out=y_all[:, e0 * C : (e0 + n) * C], in_=y_ps[:])
 
         gather(0)
         for step in range(E + 2):

@@ -18,8 +18,8 @@ ADD = mybir.AluOpType.add
 P = 128
 RAW_BUFS = 7
 PAIRED = 12
-W2_PIECES = ((0, 4), (4, 4), (8, 4), (12, 2), (14, 1), (15, 1))
-W2_EXPERTS_ON_VECTOR = (2, 2, 2, 0, 1, 1)
+W2_PIECES = ((0, 4), (4, 4), (8, 4), (12, 2), (14, 2))
+W2_EXPERTS_ON_VECTOR = (2, 2, 2, 0, 2)
 Y_WOVEN = 12
 X_C_ON_VECTOR = 160
 W1_EXPERTS_ON_SCALAR = 2
@@ -229,7 +229,7 @@ def tile_routed_moe_kernel(tc, xT, w1, w3, w2, gate, offs, pos1, pos2, out):
                         dst = y_all[:, 0 : Y_WOVEN * C].rearrange("p (k b c) -> p b k c", b=3, c=C)[:, b]
                         nc.scalar.copy(out=dst, in_=woven[b][:])
             else:
-                pool, tag = ((psum_y, "y_ps"), (psum_a, "a_ps"), (psum_b, "b_ps"))[i - 3]
+                pool, tag = ((psum_y, "y_ps"), (psum_a, "a_ps"))[i - 3]
                 y_ps = pool.tile([P, n * C], F32, name="y_last", tag=tag)
                 for k in range(n):
                     y_matmul(e0 + k, y_ps[:, k * C : (k + 1) * C])

@@ -23,6 +23,7 @@ W2_EXPERTS_ON_VECTOR = (2, 2, 2, 0, 2)
 Y_WOVEN = 12
 X_C_ON_VECTOR = 160
 W1_EXPERTS_ON_SCALAR = 2
+LAST_W3_M_ON_SCALAR = 80
 GATHER_SLOTS = 512
 OUT_CHUNK = 256
 
@@ -145,7 +146,11 @@ def tile_routed_moe_kernel(tc, xT, w1, w3, w2, gate, offs, pos1, pos2, out):
                 nc.scalar.copy(out=d1, in_=s1)
             else:
                 nc.vector.tensor_copy(out=d1, in_=s1)
-            nc.scalar.copy(out=d3, in_=s3)
+            if e >= E - 2:
+                nc.vector.tensor_copy(out=d3[:, LAST_W3_M_ON_SCALAR:P], in_=s3[:, LAST_W3_M_ON_SCALAR:P])
+                nc.scalar.copy(out=d3[:, 0:LAST_W3_M_ON_SCALAR], in_=s3[:, 0:LAST_W3_M_ON_SCALAR])
+            else:
+                nc.scalar.copy(out=d3, in_=s3)
 
         def layer1(e, half):
             cols = slice(half * H, (half + 1) * H)

@@ -98,7 +98,8 @@ def tile_routed_moe_kernel(tc, xT, w1, w3, w2, gate, offs, pos1, pos2, out):
                 raw_tiles[("w2", i)] = t
             else:
                 t = raw.tile([P, 2, T], F32, name="raw_gate", tag="raw")
-                nc.sync.dma_start(out=t[:], in_=gate.rearrange("g n t -> n g t"))
+                nc.sync.dma_start(out=t[:, 0, :], in_=gate[0])
+                nc.sync.dma_start(out=t[:, 1, :], in_=gate[1])
                 raw_tiles[("gate", 0)] = t
 
         def issue_loads(step):

@@ -24,6 +24,7 @@ Y_WOVEN = 12
 X_C_ON_VECTOR = 160
 W1_EXPERTS_ON_SCALAR = 2
 LAST_W3_M_ON_SCALAR = 80
+LAST_WOVEN_C_ON_VECTOR = 20
 GATHER_SLOTS = 512
 OUT_CHUNK = 256
 
@@ -200,6 +201,10 @@ def tile_routed_moe_kernel(tc, xT, w1, w3, w2, gate, offs, pos1, pos2, out):
             nv = W2_EXPERTS_ON_VECTOR[i]
             d = w2g[i].rearrange("p e (c i j) -> p e c j i", i=4, j=4)
             s = raw_tiles[("w2", i)].rearrange("p e (j c i) -> p e c j i", j=4, i=4)
+            if e0 + n == Y_WOVEN:
+                nc.vector.tensor_copy(out=d[:, :, 0:LAST_WOVEN_C_ON_VECTOR], in_=s[:, :, 0:LAST_WOVEN_C_ON_VECTOR])
+                nc.scalar.copy(out=d[:, :, LAST_WOVEN_C_ON_VECTOR : N // 4], in_=s[:, :, LAST_WOVEN_C_ON_VECTOR : N // 4])
+                return
             if nv > 0:
                 nc.vector.tensor_copy(out=d[:, 0:nv], in_=s[:, 0:nv])
             if nv < n:
@@ -239,10 +244,7 @@ def tile_routed_moe_kernel(tc, xT, w1, w3, w2, gate, offs, pos1, pos2, out):
                 y_ps = pool.tile([P, n * C], F32, name="y_last", tag=tag)
                 for k in range(n):
                     y_matmul(e0 + k, y_ps[:, k * C : (k + 1) * C])
-                if e0 + n == E:
-                    nc.vector.tensor_copy(out=y_all[:, e0 * C : (e0 + n) * C], in_=y_ps[:])
-                else:
-                    nc.scalar.copy(out=y_all[:, e0 * C : (e0 + n) * C], in_=y_ps[:])
+                nc.vector.tensor_copy(out=y_all[:, e0 * C : (e0 + n) * C], in_=y_ps[:])
 
         gather(0)
         for step in range(E + 2):

@@ -84,7 +84,8 @@ def tile_routed_moe_kernel(tc, xT, w1, w3, w2, gate, offs, pos1, pos2, out):
             elif kind in ("w1_pair", "w3_pair"):
                 t = raw.tile([P, 2, 4 * H], F32, name="raw_w", tag="raw")
                 src = w1 if kind == "w1_pair" else w3
-                nc.sync.dma_start(out=t[:], in_=src[2 * i : 2 * i + 2].rearrange("e (p j) c -> p e (j c)", j=4))
+                nc.sync.dma_start(out=t[:, 0, :], in_=src[2 * i].rearrange("(p j) c -> p (j c)", j=4))
+                nc.scalar.dma_start(out=t[:, 1, :], in_=src[2 * i + 1].rearrange("(p j) c -> p (j c)", j=4))
                 raw_tiles[(kind[0:2], 2 * i)] = t[:, 0, :]
                 raw_tiles[(kind[0:2], 2 * i + 1)] = t[:, 1, :]
             elif kind in ("w1", "w3"):

@@ -16,7 +16,7 @@ MULT = mybir.AluOpType.mult
 ADD = mybir.AluOpType.add
 
 P = 128
-RAW_BUFS = 7
+RAW_BUFS = 8
 PAIRED = 12
 W2_PIECES = ((0, 4), (4, 4), (8, 4), (12, 2), (14, 2))
 W2_EXPERTS_ON_VECTOR = (2, 2, 2, 0, 2)
@@ -38,7 +38,6 @@ def tile_routed_moe_kernel(tc, xT, w1, w3, w2, gate, offs, pos1, pos2, out):
         stage = ctx.enter_context(tc.tile_pool(name="stage", bufs=3))
         grouped = ctx.enter_context(tc.tile_pool(name="grouped", bufs=4))
         hidden = ctx.enter_context(tc.tile_pool(name="hidden", bufs=2))
-        fin = ctx.enter_context(tc.tile_pool(name="fin", bufs=1))
         psum_a = ctx.enter_context(tc.psum_pool(name="psum_a", bufs=2))
         psum_b = ctx.enter_context(tc.psum_pool(name="psum_b", bufs=2))
         psum_y = ctx.enter_context(tc.psum_pool(name="psum_y", bufs=4))
@@ -272,11 +271,10 @@ def tile_routed_moe_kernel(tc, xT, w1, w3, w2, gate, offs, pos1, pos2, out):
                 layer2(i - 1)
 
         gate_t = raw_tiles[("gate", 0)]
-        g1 = fin.tile([P, T], F32, name="g1", tag="g1")
-        g2 = fin.tile([P, T], F32, name="g2", tag="g2")
-        res = fin.tile([P, T], F32, name="res", tag="res")
-        nc.vector.tensor_tensor(out=g1[:], in0=y_all[:].indirect(pos1_t[:]), in1=gate_t[:, 0, :], op=MULT)
-        nc.vector.tensor_tensor(out=g2[:], in0=y_all[:].indirect(pos2_t[:]), in1=gate_t[:, 1, :], op=MULT)
+        fin = raw.tile([P, 3, T], F32, name="fin", tag="raw")
+        g1, g2, res = fin[:, 0, :], fin[:, 1, :], fin[:, 2, :]
+        nc.vector.tensor_tensor(out=g1, in0=y_all[:].indirect(pos1_t[:]), in1=gate_t[:, 0, :], op=MULT)
+        nc.vector.tensor_tensor(out=g2, in0=y_all[:].indirect(pos2_t[:]), in1=gate_t[:, 1, :], op=MULT)
         for c in range(T // OUT_CHUNK):
             tok = slice(c * OUT_CHUNK, (c + 1) * OUT_CHUNK)
             nc.vector.tensor_tensor(out=res[:, tok], in0=g1[:, tok], in1=g2[:, tok], op=ADD)

from contextlib import ExitStack

import concourse.mybir as mybir

K, T, E, C, H, N = 512, 1024, 16, 128, 512, 128
FLOPS = 2 * E * C * (2 * K * H + H * N)

F32 = mybir.dt.float32
BF16 = mybir.dt.bfloat16
U32 = mybir.dt.uint32
U16 = mybir.dt.uint16
U8 = mybir.dt.uint8
FP8X4 = mybir.dt.float8_e4m3fn_x4
SILU = mybir.ActivationFunctionType.Silu
MULT = mybir.AluOpType.mult
ADD = mybir.AluOpType.add

P = 128
RAW_BUFS = 8
PAIRED = 12
W2_PIECES = ((0, 4), (4, 4), (8, 4), (12, 2), (14, 2))
W2_EXPERTS_ON_VECTOR = (2, 2, 2, 0, 2)
Y_WOVEN = 12
X_C_ON_VECTOR = 160
W1_EXPERTS_ON_SCALAR = 2
LAST_W3_M_ON_SCALAR = 80
LAST_WOVEN_C_ON_VECTOR = 20
GATHER_SLOTS = 512
OUT_CHUNK = 256


def tile_routed_moe_kernel(tc, xT, w1, w3, w2, gate, offs, pos1, pos2, out):
    nc = tc.nc
    with ExitStack() as ctx:
        lists = ctx.enter_context(tc.tile_pool(name="lists", bufs=1))
        keep = ctx.enter_context(tc.tile_pool(name="keep", bufs=1))
        raw = ctx.enter_context(tc.tile_pool(name="raw", bufs=RAW_BUFS))
        stage = ctx.enter_context(tc.tile_pool(name="stage", bufs=3))
        grouped = ctx.enter_context(tc.tile_pool(name="grouped", bufs=4))
        hidden = ctx.enter_context(tc.tile_pool(name="hidden", bufs=2))
        psum_a = ctx.enter_context(tc.psum_pool(name="psum_a", bufs=2))
        psum_b = ctx.enter_context(tc.psum_pool(name="psum_b", bufs=2))
        psum_y = ctx.enter_context(tc.psum_pool(name="psum_y", bufs=4))

        offs_t = lists.tile([P, E * C // 16], U16, name="offs_t")
        pos1_t = lists.tile([P, T // 16], U16, name="pos1_t")
        pos2_t = lists.tile([P, T // 16], U16, name="pos2_t")

        x_words = keep.tile([P, T], U32, name="x_words", align_bytes=64)
        x_bytes = keep.tile([P, T], U8, name="x_bytes", align_bytes=64)
        xg_words = keep.tile([P, E * C], U32, name="xg_words", align_bytes=64)
        xg_bytes = keep.tile([P, E * C], U8, name="xg_bytes", align_bytes=64)
        h_words = keep.tile([P, E * C], U32, name="h_words", align_bytes=64)
        h_bytes = keep.tile([P, E * C], U8, name="h_bytes", align_bytes=64)
        w2_words = keep.tile([P, E * N], U32, name="w2_words", align_bytes=64)
        w2_bytes = keep.tile([P, E * N], U8, name="w2_bytes", align_bytes=64)
        y_all = keep.tile([P, E * C], F32, name="y_all")
        zero_col = keep.tile([P, 1], F32, name="zero_col")
        silu_col = keep.tile([P, 1], F32, name="silu_col")

        nc.vector.memset(zero_col[:], 0.0)
        nc.scalar.activation(out=silu_col[:], in_=zero_col[:], func=SILU)
        nc.gpsimd.memset(x_bytes[:], 0)

        raw_tiles = {}
        jobs = [("x", 0, -1)]
        for i in range(PAIRED // 2):
            jobs.append(("w1_pair", i, 2 * i + 1))
            jobs.append(("w3_pair", i, 2 * i + 3))
        for e in range(PAIRED, E):
            jobs.append(("w1", e, e))
            jobs.append(("w3", e, e + 2))
        for i in range(len(W2_PIECES)):
            jobs.append(("w2", i, E + 2))
        jobs.append(("gate", 0, E + 2))
        issued = [0]

        def load(kind, i):
            if kind == "x":
                t = raw.tile([P, 4, T], F32, name="raw_x", tag="raw")
                nc.sync.dma_start(out=t[:], in_=xT.rearrange("(p j) n -> p j n", j=4))
                raw_tiles[("x", 0)] = t
            elif kind in ("w1_pair", "w3_pair"):
                t = raw.tile([P, 2, 4 * H], F32, name="raw_w", tag="raw")
                src = w1 if kind == "w1_pair" else w3
                nc.sync.dma_start(out=t[:, 0, :], in_=src[2 * i].rearrange("(p j) c -> p (j c)", j=4))
                nc.scalar.dma_start(out=t[:, 1, :], in_=src[2 * i + 1].rearrange("(p j) c -> p (j c)", j=4))
                raw_tiles[(kind[0:2], 2 * i)] = t[:, 0, :]
                raw_tiles[(kind[0:2], 2 * i + 1)] = t[:, 1, :]
            elif kind in ("w1", "w3"):
                t = raw.tile([P, 4 * H], F32, name="raw_w_one", tag="raw")
                src = w1 if kind == "w1" else w3
                nc.sync.dma_start(out=t[:], in_=src[i].rearrange("(p j) c -> p (j c)", j=4))
                raw_tiles[(kind, i)] = t
            elif kind == "w2":
                e0, n = W2_PIECES[i]
                t = raw.tile([P, n, 4 * N], F32, name="raw_w2", tag="raw")
                nc.sync.dma_start(out=t[:], in_=w2[e0 : e0 + n].rearrange("e (p j) n -> p e (j n)", j=4))
                raw_tiles[("w2", i)] = t
            else:
                t = raw.tile([P, 2, T], F32, name="raw_gate", tag="raw")
                nc.sync.dma_start(out=t[:, 0, :], in_=gate[0])
                nc.sync.dma_start(out=t[:, 1, :], in_=gate[1])
                raw_tiles[("gate", 0)] = t

        def issue_loads(step):
            while issued[0] < len(jobs) and (issued[0] < RAW_BUFS or jobs[issued[0] - RAW_BUFS][2] < step):
                load(jobs[issued[0]][0], jobs[issued[0]][1])
                issued[0] += 1

        nc.sync.dma_start(out=offs_t[:], in_=offs)
        load("x", 0)
        issued[0] = 1
        nc.sync.dma_start(out=pos1_t[:], in_=pos1)
        nc.sync.dma_start(out=pos2_t[:], in_=pos2)
        issue_loads(-1)

        x_grp = grouped.tile([P, T, 4], BF16, name="x_grp", tag="wg", align_bytes=64)
        x_dst = x_grp.rearrange("p (c i) j -> p c j i", i=4)
        x_src = raw_tiles[("x", 0)].rearrange("p j (c i) -> p c j i", i=4)
        nc.vector.tensor_copy(out=x_dst[:, 0:128], in_=x_src[:, 0:128])
        nc.vector.tensor_copy(out=x_dst[:, 128:X_C_ON_VECTOR], in_=x_src[:, 128:X_C_ON_VECTOR])
        nc.scalar.copy(out=x_dst[:, X_C_ON_VECTOR:256], in_=x_src[:, X_C_ON_VECTOR:256])
        for c in range(2):
            nc.vector.quantize_mx(
                out=x_words[:, 512 * c : 512 * (c + 1)].bitcast(FP8X4),
                scales=x_bytes[:, 512 * c : 512 * (c + 1)],
                in_=x_grp[:, 512 * c : 512 * (c + 1), :].rearrange("p n j -> p (n j)"),
            )

        def gather(q):
            cols = slice(q * GATHER_SLOTS // 16, (q + 1) * GATHER_SLOTS // 16)
            slots = slice(q * GATHER_SLOTS, (q + 1) * GATHER_SLOTS)
            nc.vector.tensor_copy(out=xg_words[:, slots], in_=x_words[:].indirect(offs_t[:, cols]))
            nc.vector.tensor_copy(out=xg_bytes[:, slots], in_=x_bytes[:].indirect(offs_t[:, cols]))

        wg, wc, ws, acc, sa, hb = {}, {}, {}, {}, {}, {}

        def interleave_w(e):
            wg[e] = grouped.tile([P, 2, 4 * H], BF16, name="wg", tag="wg", align_bytes=64)
            wc[e] = stage.tile([P, 2 * H], U32, name="wc", tag="wc", align_bytes=64)
            ws[e] = stage.tile([P, 2 * H], U8, name="ws", tag="ws", align_bytes=64)
            d1 = wg[e][:, 0, :].rearrange("p (t m j) -> p m j t", t=4, j=4)
            s1 = raw_tiles[("w1", e)].rearrange("p (j m t) -> p m j t", j=4, t=4)
            d3 = wg[e][:, 1, :].rearrange("p (t m j) -> p m j t", t=4, j=4)
            s3 = raw_tiles[("w3", e)].rearrange("p (j m t) -> p m j t", j=4, t=4)
            if e < W1_EXPERTS_ON_SCALAR:
                nc.scalar.copy(out=d1, in_=s1)
            else:
                nc.vector.tensor_copy(out=d1, in_=s1)
            if e >= E - 2:
                nc.vector.tensor_copy(out=d3[:, LAST_W3_M_ON_SCALAR:P], in_=s3[:, LAST_W3_M_ON_SCALAR:P])
                nc.scalar.copy(out=d3[:, 0:LAST_W3_M_ON_SCALAR], in_=s3[:, 0:LAST_W3_M_ON_SCALAR])
            else:
                nc.scalar.copy(out=d3, in_=s3)

        def layer1(e, half):
            cols = slice(half * H, (half + 1) * H)
            nc.vector.quantize_mx(out=wc[e][:, cols].bitcast(FP8X4), scales=ws[e][:, cols], in_=wg[e][:, half, :])
            slots = slice(e * C, (e + 1) * C)
            if half == 0:
                acc[(e, half)] = psum_a.tile([P, 4, C], F32, name="a_ps", tag="a_ps")
            else:
                acc[(e, half)] = psum_b.tile([P, 4, C], F32, name="b_ps", tag="b_ps")
            for t in range(4):
                cols = slice(half * H + t * P, half * H + (t + 1) * P)
                nc.tensor.matmul_mx(
                    out=acc[(e, half)][:, t, :],
                    lhsT=wc[e][:, cols].bitcast(FP8X4),
                    lhsT_scale=ws[e][:, cols],
                    rhs=xg_words[:, slots].bitcast(FP8X4),
                    rhs_scale=xg_bytes[:, slots],
                    start=True,
                    stop=True,
                )

        def silu(e):
            sa[e] = raw_tiles[("w3", e)][:, 0 : 4 * C].rearrange("p (s t) -> p s t", t=4)
            nc.scalar.activation(out=sa[e], in_=acc[(e, 0)].rearrange("p t s -> p s t"), func=SILU)

        def product(e):
            if e % 2 == 0:
                hb[e // 2] = hidden.tile([P, 8 * C], BF16, name="hb", tag="hb", align_bytes=64)
            k = e % 2
            nc.vector.tensor_tensor(
                out=hb[e // 2][:, 4 * C * k : 4 * C * (k + 1)].rearrange("p (s t) -> p s t", t=4),
                in0=sa[e],
                in1=acc[(e, 1)].rearrange("p t s -> p s t"),
                op=MULT,
            )

        def quant_h(i):
            slots = slice(2 * i * C, (2 * i + 2) * C)
            nc.vector.quantize_mx(out=h_words[:, slots].bitcast(FP8X4), scales=h_bytes[:, slots], in_=hb[i][:])

        w2g = {}

        def interleave_w2(i):
            e0, n = W2_PIECES[i]
            w2g[i] = stage.tile([P, n, 4 * N], BF16, name="w2g", tag="w2g", align_bytes=64)
            nv = W2_EXPERTS_ON_VECTOR[i]
            d = w2g[i].rearrange("p e (c i j) -> p e c j i", i=4, j=4)
            s = raw_tiles[("w2", i)].rearrange("p e (j c i) -> p e c j i", j=4, i=4)
            if e0 + n == Y_WOVEN:
                nc.vector.tensor_copy(out=d[:, :, 0:LAST_WOVEN_C_ON_VECTOR], in_=s[:, :, 0:LAST_WOVEN_C_ON_VECTOR])
                nc.scalar.copy(out=d[:, :, LAST_WOVEN_C_ON_VECTOR : N // 4], in_=s[:, :, LAST_WOVEN_C_ON_VECTOR : N // 4])
                return
            if nv > 0:
                nc.vector.tensor_copy(out=d[:, 0:nv], in_=s[:, 0:nv])
            if nv < n:
                nc.scalar.copy(out=d[:, nv:n], in_=s[:, nv:n])

        def y_matmul(e, where):
            sl = slice(e * C, (e + 1) * C)
            nc.tensor.matmul_mx(
                out=where,
                lhsT=w2_words[:, sl].bitcast(FP8X4),
                lhsT_scale=w2_bytes[:, sl],
                rhs=h_words[:, sl].bitcast(FP8X4),
                rhs_scale=h_bytes[:, sl],
                start=True,
                stop=True,
            )

        woven = []
        for b in range(3):
            woven.append(psum_y.tile([P, 4, C], F32, name="y_woven", tag="y_ps"))

        def layer2(i):
            e0, n = W2_PIECES[i]
            cols = slice(e0 * N, (e0 + n) * N)
            nc.vector.quantize_mx(
                out=w2_words[:, cols].bitcast(FP8X4), scales=w2_bytes[:, cols], in_=w2g[i].rearrange("p e c -> p (e c)")
            )
            if e0 < Y_WOVEN:
                for e in range(e0, e0 + n):
                    y_matmul(e, woven[e % 3][:, e // 3, :])
                if e0 + n == Y_WOVEN:
                    for b in range(3):
                        dst = y_all[:, 0 : Y_WOVEN * C].rearrange("p (k b c) -> p b k c", b=3, c=C)[:, b]
                        nc.scalar.copy(out=dst, in_=woven[b][:])
            else:
                pool, tag = ((psum_y, "y_ps"), (psum_a, "a_ps"))[i - 3]
                y_ps = pool.tile([P, n * C], F32, name="y_last", tag=tag)
                for k in range(n):
                    y_matmul(e0 + k, y_ps[:, k * C : (k + 1) * C])
                nc.vector.tensor_copy(out=y_all[:, e0 * C : (e0 + n) * C], in_=y_ps[:])

        gather(0)
        for step in range(E + 2):
            issue_loads(step)
            if step < E:
                interleave_w(step)
            if step % 4 == 1 and step // 4 + 1 < 4:
                gather(step // 4 + 1)
            if step < E:
                layer1(step, 0)
            if 0 <= step - 1 < E:
                silu(step - 1)
                layer1(step - 1, 1)
            if 0 <= step - 2 < E:
                product(step - 2)
                if step % 2 == 1:
                    quant_h((step - 2) // 2)
        issue_loads(E + 3)

        for i in range(len(W2_PIECES) + 1):
            if i < len(W2_PIECES):
                interleave_w2(i)
            if i > 0:
                layer2(i - 1)

        gate_t = raw_tiles[("gate", 0)]
        fin = raw.tile([P, 3, T], F32, name="fin", tag="raw")
        g1, g2, res = fin[:, 0, :], fin[:, 1, :], fin[:, 2, :]
        nc.vector.tensor_tensor(out=g1, in0=y_all[:].indirect(pos1_t[:]), in1=gate_t[:, 0, :], op=MULT)
        nc.vector.tensor_tensor(out=g2, in0=y_all[:].indirect(pos2_t[:]), in1=gate_t[:, 1, :], op=MULT)
        for c in range(T // OUT_CHUNK):
            tok = slice(c * OUT_CHUNK, (c + 1) * OUT_CHUNK)
            nc.vector.tensor_tensor(out=res[:, tok], in0=g1[:, tok], in1=g2[:, tok], op=ADD)
            nc.sync.dma_start(out=out[:, tok], in_=res[:, tok])
